import numpy as np
import ml_dtypes

BF16 = ml_dtypes.bfloat16


def bf(x):
    return np.asarray(x, np.float32).astype(BF16)


def f32(x):
    return np.asarray(x, np.float32)


def f64(x):
    return np.asarray(x).astype(np.float64)


def striped(idx):
    return np.tile(idx.reshape(-1, 16).T, (8, 1))


def rows(idx, k):
    return np.tile(idx, (k, 1))


def look(tab, idx):
    return np.take_along_axis(f64(tab), rows(idx, len(tab)), axis=1)


K, S, V, N, M = 512, 256, 128, 128, 256


def setup_inputs():
    return {"tab": f32(np.random.standard_normal((K, S))), "s": f32(np.random.uniform(0.5, 1.5, (K, 1))), "c": f32(0.3 * np.random.standard_normal((K, 1))), "w": bf(np.random.standard_normal((K, M)) / np.sqrt(K)), "offs": striped(np.random.randint(0, S, N))}


def reference(tab, s, c, w, offs):
    idx = offs[:16].T.reshape(-1)
    t = look(tab, idx)
    x = f64(s) * t + f64(c)
    y = f64(w).T @ x
    return y

@@ -1,0 +1,66 @@
+import concourse.mybir as mybir
+
+F32, BF16, U16 = mybir.dt.float32, mybir.dt.bfloat16, mybir.dt.uint16
+MULT, ADD = mybir.AluOpType.mult, mybir.AluOpType.add
+
+P = 128
+K, S, N, M = 512, 256, 128, 256
+BLOCKS = K // P
+HALVES = M // P
+
+FLOPS = 2 * K * M * N
+
+
+def tile_lookup_deq_affp_none_kernel(tc, tab, s, c, w, offs, out):
+    nc = tc.nc
+
+    tab_blocks = tab.rearrange("(p b) t -> b p t", b=BLOCKS)
+    s_rows = s.rearrange("(p b) one -> p (b one)", b=BLOCKS)
+    c_rows = c.rearrange("(p b) one -> p (b one)", b=BLOCKS)
+    w_rows = w.rearrange("(p b) m -> p (b m)", b=BLOCKS)
+
+    with (
+        tc.tile_pool(name="held", bufs=1) as held,
+        tc.psum_pool(name="psum", bufs=1) as psum,
+    ):
+        offsets = held.tile([P, N // 16], U16, name="offsets")
+        scale = held.tile([P, BLOCKS], F32, name="scale")
+        shift = held.tile([P, BLOCKS], F32, name="shift")
+        weights = held.tile([P, BLOCKS * M], BF16, name="weights")
+        windows = [held.tile([P, S], F32, name=f"window{b}") for b in range(BLOCKS)]
+
+        nc.sync.dma_start(offsets[:], offs)
+        nc.scalar.dma_start(scale[:], s_rows)
+        nc.scalar.dma_start(shift[:], c_rows)
+        nc.gpsimd.dma_start(weights[:], w_rows)
+        for b in range(BLOCKS):
+            queue = nc.sync if b % 2 == 0 else nc.scalar
+            queue.dma_start(windows[b][:], tab_blocks[b])
+
+        products = [psum.tile([P, N], F32, name=f"product{h}") for h in range(HALVES)]
+        for b in range(BLOCKS):
+            x = held.tile([P, N], F32, name=f"x{b}")
+            nc.vector.tensor_scalar(
+                x[:],
+                windows[b][:].indirect(offsets[:]),
+                scale[:, b : b + 1],
+                shift[:, b : b + 1],
+                op0=MULT,
+                op1=ADD,
+            )
+            x_bf16 = held.tile([P, N], BF16, name=f"x_bf16_{b}")
+            nc.scalar.copy(x_bf16[:], x[:])
+            for h in range(HALVES):
+                nc.tensor.matmul(
+                    products[h][:],
+                    weights[:, b * M + h * P : b * M + (h + 1) * P],
+                    x_bf16[:],
+                    start=b == 0,
+                    stop=b == BLOCKS - 1,
+                )
+
+        results = [held.tile([P, N], F32, name=f"result{h}") for h in range(HALVES)]
+        nc.vector.tensor_copy(results[0][:], products[0][:])
+        nc.sync.dma_start(out[0:P, :], results[0][:])
+        nc.scalar.copy(results[1][:], products[1][:])
+        nc.scalar.dma_start(out[P:M, :], results[1][:])

@@ -6,6 +6,8 @@ MULT, ADD = mybir.AluOpType.mult, mybir.AluOpType.add
 P = 128
 K, S, N, M = 512, 256, 128, 256
 BLOCKS = K // P
+WARM_COLUMNS = 512
+WARM_MATMULS = 6
 HALVES = M // P
 
 FLOPS = 2 * K * M * N
@@ -36,6 +38,12 @@ def tile_lookup_deq_affp_none_kernel(tc, tab, s, c, w, offs, out):
         for b in range(BLOCKS):
             queue = nc.sync if b % 2 == 0 else nc.scalar
             queue.dma_start(windows[b][:], tab_blocks[b])
+
+        zeros = held.tile([P, WARM_COLUMNS], BF16, name="zeros")
+        nc.vector.memset(zeros[:], 0.0)
+        unread = psum.tile([P, WARM_COLUMNS], F32, name="unread")
+        for turn in range(WARM_MATMULS):
+            nc.tensor.matmul(unread[:], zeros[:, 0:P], zeros[:], start=True, stop=True)
 
         products = [psum.tile([P, N], F32, name=f"product{h}") for h in range(HALVES)]
         for b in range(BLOCKS):

@@ -57,7 +57,10 @@ def tile_lookup_deq_affp_none_kernel(tc, tab, s, c, w, offs, out):
                 op1=ADD,
             )
             x_bf16 = held.tile([P, N], BF16, name=f"x_bf16_{b}")
-            nc.scalar.copy(x_bf16[:], x[:])
+            if b < BLOCKS - 1:
+                nc.scalar.copy(x_bf16[:], x[:])
+            else:
+                nc.vector.tensor_copy(x_bf16[:], x[:])
             for h in range(HALVES):
                 nc.tensor.matmul(
                     products[h][:],

import concourse.mybir as mybir

F32, BF16, U16 = mybir.dt.float32, mybir.dt.bfloat16, mybir.dt.uint16
MULT, ADD = mybir.AluOpType.mult, mybir.AluOpType.add

P = 128
K, S, N, M = 512, 256, 128, 256
BLOCKS = K // P
WARM_COLUMNS = 512
WARM_MATMULS = 6
HALVES = M // P

FLOPS = 2 * K * M * N


def tile_lookup_deq_affp_none_kernel(tc, tab, s, c, w, offs, out):
    nc = tc.nc

    tab_blocks = tab.rearrange("(p b) t -> b p t", b=BLOCKS)
    s_rows = s.rearrange("(p b) one -> p (b one)", b=BLOCKS)
    c_rows = c.rearrange("(p b) one -> p (b one)", b=BLOCKS)
    w_rows = w.rearrange("(p b) m -> p (b m)", b=BLOCKS)

    with (
        tc.tile_pool(name="held", bufs=1) as held,
        tc.psum_pool(name="psum", bufs=1) as psum,
    ):
        offsets = held.tile([P, N // 16], U16, name="offsets")
        scale = held.tile([P, BLOCKS], F32, name="scale")
        shift = held.tile([P, BLOCKS], F32, name="shift")
        weights = held.tile([P, BLOCKS * M], BF16, name="weights")
        windows = [held.tile([P, S], F32, name=f"window{b}") for b in range(BLOCKS)]

        nc.sync.dma_start(offsets[:], offs)
        nc.scalar.dma_start(scale[:], s_rows)
        nc.scalar.dma_start(shift[:], c_rows)
        nc.gpsimd.dma_start(weights[:], w_rows)
        for b in range(BLOCKS):
            queue = nc.sync if b % 2 == 0 else nc.scalar
            queue.dma_start(windows[b][:], tab_blocks[b])

        zeros = held.tile([P, WARM_COLUMNS], BF16, name="zeros")
        nc.vector.memset(zeros[:], 0.0)
        unread = psum.tile([P, WARM_COLUMNS], F32, name="unread")
        for turn in range(WARM_MATMULS):
            nc.tensor.matmul(unread[:], zeros[:, 0:P], zeros[:], start=True, stop=True)

        products = [psum.tile([P, N], F32, name=f"product{h}") for h in range(HALVES)]
        for b in range(BLOCKS):
            x = held.tile([P, N], F32, name=f"x{b}")
            nc.vector.tensor_scalar(
                x[:],
                windows[b][:].indirect(offsets[:]),
                scale[:, b : b + 1],
                shift[:, b : b + 1],
                op0=MULT,
                op1=ADD,
            )
            x_bf16 = held.tile([P, N], BF16, name=f"x_bf16_{b}")
            if b < BLOCKS - 1:
                nc.scalar.copy(x_bf16[:], x[:])
            else:
                nc.vector.tensor_copy(x_bf16[:], x[:])
            for h in range(HALVES):
                nc.tensor.matmul(
                    products[h][:],
                    weights[:, b * M + h * P : b * M + (h + 1) * P],
                    x_bf16[:],
                    start=b == 0,
                    stop=b == BLOCKS - 1,
                )

        results = [held.tile([P, N], F32, name=f"result{h}") for h in range(HALVES)]
        nc.vector.tensor_copy(results[0][:], products[0][:])
        nc.sync.dma_start(out[0:P, :], results[0][:])
        nc.scalar.copy(results[1][:], products[1][:])
        nc.scalar.dma_start(out[P:M, :], results[1][:])
